import numpy as np
import ml_dtypes

BF16 = ml_dtypes.bfloat16


def bf(x):
    return np.asarray(x, np.float32).astype(BF16)


def f32(x):
    return np.asarray(x, np.float32)


def f64(x):
    return np.asarray(x).astype(np.float64)


def striped(idx):
    return np.tile(idx.reshape(-1, 16).T, (8, 1))


S, K, M, N = 256, 128, 256, 192


def setup_inputs():
    return {"base": bf(np.random.standard_normal((M, S))), "x": bf(np.random.standard_normal((K, N))), "w": bf(np.random.standard_normal((K, M)) / np.sqrt(K)), "c": f32(0.2 + 0.8 * np.random.random_sample((1, S))), "offs": striped(np.random.permutation(S)[:N])}


def reference(base, x, w, c, offs):
    idx = offs[:16].T.reshape(-1)
    z = f64(base).copy()
    z[:, idx] += f64(w).T @ f64(x)
    return z * f64(c)

@@ -1,0 +1,55 @@
+import concourse.mybir as mybir
+from concourse.masks import make_identity
+
+BF16 = mybir.dt.bfloat16
+F32 = mybir.dt.float32
+U16 = mybir.dt.uint16
+MULT = mybir.AluOpType.mult
+
+P = 128
+FLOPS = 2 * 128 * 256 * 192
+
+
+def tile_scatter_matmul_kernel(tc, base, x, w, c, offs, out):
+    nc = tc.nc
+    features, tokens = base.shape
+    picked = x.shape[1]
+    blocks = features // P
+
+    with (
+        tc.tile_pool(name="held", bufs=1) as held,
+        tc.psum_pool(name="windows", bufs=1) as windows,
+    ):
+        identity = held.tile([P, P], BF16)
+        base_tile = held.tile([P, blocks, tokens], BF16)
+        offsets = held.tile([P, picked // 16], U16)
+        w_tile = held.tile([P, features], BF16)
+        x_tile = held.tile([P, picked], BF16)
+        c_tile = held.tile([P, tokens], F32)
+
+        nc.sync.dma_start(base_tile[:], base.rearrange("(a p) t -> p a t", p=P))
+        nc.sync.dma_start(offsets[:], offs)
+        nc.sync.dma_start(w_tile[:], w)
+        nc.sync.dma_start(x_tile[:], x)
+        nc.sync.dma_start(c_tile[:], c.rearrange("o t -> (o t)").partition_broadcast(P))
+        make_identity(nc, identity[:])
+
+        window_tiles = []
+        for a in range(blocks):
+            window = windows.tile([P, tokens], F32, name=f"window{a}")
+            nc.tensor.matmul(window[:], identity[:], base_tile[:, a, :], start=True, stop=False)
+            window_tiles.append(window)
+
+        for a, window in enumerate(window_tiles):
+            nc.tensor.matmul(
+                window[:].indirect(offsets[:]),
+                w_tile[:, a * P : (a + 1) * P],
+                x_tile[:],
+                start=False,
+                stop=True,
+            )
+
+        for a, window in enumerate(window_tiles):
+            scaled = held.tile([P, tokens], F32, name=f"scaled{a}")
+            nc.vector.tensor_tensor(scaled[:], window[:], c_tile[:], MULT)
+            nc.sync.dma_start(out[a * P : (a + 1) * P, :], scaled[:])

@@ -7,6 +7,8 @@ U16 = mybir.dt.uint16
 MULT = mybir.AluOpType.mult
 
 P = 128
+BANK = 512
+WARM_UP = 4
 FLOPS = 2 * 128 * 256 * 192
 
 
@@ -33,6 +35,12 @@ def tile_scatter_matmul_kernel(tc, base, x, w, c, offs, out):
         nc.sync.dma_start(x_tile[:], x)
         nc.sync.dma_start(c_tile[:], c.rearrange("o t -> (o t)").partition_broadcast(P))
         make_identity(nc, identity[:])
+
+        zeros = held.tile([P, BANK], BF16)
+        nc.vector.memset(zeros[:], 0.0)
+        spare = windows.tile([P, BANK], F32)
+        for turn in range(WARM_UP):
+            nc.tensor.matmul(spare[:], zeros[:, :P], zeros[:], start=True, stop=True)
 
         window_tiles = []
         for a in range(blocks):

@@ -7,8 +7,7 @@ U16 = mybir.dt.uint16
 MULT = mybir.AluOpType.mult
 
 P = 128
-BANK = 512
-WARM_UP = 4
+WARM_UP = 6
 FLOPS = 2 * 128 * 256 * 192
 
 
@@ -36,9 +35,9 @@ def tile_scatter_matmul_kernel(tc, base, x, w, c, offs, out):
         nc.sync.dma_start(c_tile[:], c.rearrange("o t -> (o t)").partition_broadcast(P))
         make_identity(nc, identity[:])
 
-        zeros = held.tile([P, BANK], BF16)
+        zeros = held.tile([P, tokens], BF16)
         nc.vector.memset(zeros[:], 0.0)
-        spare = windows.tile([P, BANK], F32)
+        spare = windows.tile([P, tokens], F32)
         for turn in range(WARM_UP):
             nc.tensor.matmul(spare[:], zeros[:, :P], zeros[:], start=True, stop=True)
 

@@ -26,13 +26,15 @@ def tile_scatter_matmul_kernel(tc, base, x, w, c, offs, out):
         offsets = held.tile([P, picked // 16], U16)
         w_tile = held.tile([P, features], BF16)
         x_tile = held.tile([P, picked], BF16)
+        c_row = held.tile([1, tokens], F32)
+        ones = held.tile([1, P], F32)
         c_tile = held.tile([P, tokens], F32)
 
+        nc.sync.dma_start(c_row[:], c)
         nc.sync.dma_start(base_tile[:], base.rearrange("(a p) t -> p a t", p=P))
         nc.sync.dma_start(offsets[:], offs)
         nc.sync.dma_start(w_tile[:], w)
         nc.sync.dma_start(x_tile[:], x)
-        nc.sync.dma_start(c_tile[:], c.rearrange("o t -> (o t)").partition_broadcast(P))
         make_identity(nc, identity[:])
 
         zeros = held.tile([P, tokens], BF16)
@@ -40,6 +42,11 @@ def tile_scatter_matmul_kernel(tc, base, x, w, c, offs, out):
         spare = windows.tile([P, tokens], F32)
         for turn in range(WARM_UP):
             nc.tensor.matmul(spare[:], zeros[:, :P], zeros[:], start=True, stop=True)
+
+        nc.vector.memset(ones[:], 1.0)
+        c_bank = windows.tile([P, tokens], F32)
+        nc.tensor.matmul(c_bank[:], ones[:], c_row[:], start=True, stop=True)
+        nc.vector.tensor_copy(c_tile[:], c_bank[:])
 
         window_tiles = []
         for a in range(blocks):

import concourse.mybir as mybir
from concourse.masks import make_identity

BF16 = mybir.dt.bfloat16
F32 = mybir.dt.float32
U16 = mybir.dt.uint16
MULT = mybir.AluOpType.mult

P = 128
WARM_UP = 6
FLOPS = 2 * 128 * 256 * 192


def tile_scatter_matmul_kernel(tc, base, x, w, c, offs, out):
    nc = tc.nc
    features, tokens = base.shape
    picked = x.shape[1]
    blocks = features // P

    with (
        tc.tile_pool(name="held", bufs=1) as held,
        tc.psum_pool(name="windows", bufs=1) as windows,
    ):
        identity = held.tile([P, P], BF16)
        base_tile = held.tile([P, blocks, tokens], BF16)
        offsets = held.tile([P, picked // 16], U16)
        w_tile = held.tile([P, features], BF16)
        x_tile = held.tile([P, picked], BF16)
        c_row = held.tile([1, tokens], F32)
        ones = held.tile([1, P], F32)
        c_tile = held.tile([P, tokens], F32)

        nc.sync.dma_start(c_row[:], c)
        nc.sync.dma_start(base_tile[:], base.rearrange("(a p) t -> p a t", p=P))
        nc.sync.dma_start(offsets[:], offs)
        nc.sync.dma_start(w_tile[:], w)
        nc.sync.dma_start(x_tile[:], x)
        make_identity(nc, identity[:])

        zeros = held.tile([P, tokens], BF16)
        nc.vector.memset(zeros[:], 0.0)
        spare = windows.tile([P, tokens], F32)
        for turn in range(WARM_UP):
            nc.tensor.matmul(spare[:], zeros[:, :P], zeros[:], start=True, stop=True)

        nc.vector.memset(ones[:], 1.0)
        c_bank = windows.tile([P, tokens], F32)
        nc.tensor.matmul(c_bank[:], ones[:], c_row[:], start=True, stop=True)
        nc.vector.tensor_copy(c_tile[:], c_bank[:])

        window_tiles = []
        for a in range(blocks):
            window = windows.tile([P, tokens], F32, name=f"window{a}")
            nc.tensor.matmul(window[:], identity[:], base_tile[:, a, :], start=True, stop=False)
            window_tiles.append(window)

        for a, window in enumerate(window_tiles):
            nc.tensor.matmul(
                window[:].indirect(offsets[:]),
                w_tile[:, a * P : (a + 1) * P],
                x_tile[:],
                start=False,
                stop=True,
            )

        for a, window in enumerate(window_tiles):
            scaled = held.tile([P, tokens], F32, name=f"scaled{a}")
            nc.vector.tensor_tensor(scaled[:], window[:], c_tile[:], MULT)
            nc.sync.dma_start(out[a * P : (a + 1) * P, :], scaled[:])
